import numpy as np
import ml_dtypes

BF16 = ml_dtypes.bfloat16


def bf(x):
    return np.asarray(x, np.float32).astype(BF16)


def f32(x):
    return np.asarray(x, np.float32)


def f64(x):
    return np.asarray(x).astype(np.float64)


def striped(idx):
    return np.tile(idx.reshape(-1, 16).T, (8, 1))


S, K, M, N = 256, 512, 128, 128


def setup_inputs():
    return {"base": bf(np.random.standard_normal((M, S))), "x": bf(np.random.standard_normal((K, N))), "w": bf(np.random.standard_normal((K, M)) / np.sqrt(K)), "b": f32(0.5 * np.random.standard_normal((M, 1))), "offs": striped(np.random.permutation(S)[:N])}


def reference(base, x, w, b, offs):
    idx = offs[:16].T.reshape(-1)
    z = f64(base).copy()
    z[:, idx] += f64(w).T @ f64(x)
    return np.tanh(z + f64(b))

@@ -1,0 +1,46 @@
+import concourse.mybir as mybir
+from concourse.masks import make_identity
+
+P = 128
+S, K, M, N = 256, 512, 128, 128
+KB = K // P
+FLOPS = 2 * K * M * N
+
+BF16, F32, U16 = mybir.dt.bfloat16, mybir.dt.float32, mybir.dt.uint16
+TANH = mybir.ActivationFunctionType.Tanh
+
+
+def tile_scatter_matmul_kernel(tc, base, x, w, b, offs, out):
+    nc = tc.nc
+    with tc.tile_pool(name="held", bufs=1) as held, tc.psum_pool(name="psum", bufs=1) as psum:
+        offsets = held.tile([P, N // 16], U16, name="offsets")
+        nc.sync.dma_start(offsets[:], offs)
+
+        base_tile = held.tile([P, S], BF16, name="base_tile")
+        nc.scalar.dma_start(base_tile[:], base)
+        bias = held.tile([P, 1], F32, name="bias")
+        nc.scalar.dma_start(bias[:], b)
+
+        x_tile = held.tile([P, KB * N], BF16, name="x_tile")
+        nc.sync.dma_start(x_tile[:], x.rearrange("(p kb) n -> p (kb n)", kb=KB))
+        w_tile = held.tile([P, KB * M], BF16, name="w_tile")
+        nc.scalar.dma_start(w_tile[:], w.rearrange("(p kb) m -> p (kb m)", kb=KB))
+
+        identity = held.tile([P, P], BF16, name="identity")
+        make_identity(nc, identity[:])
+
+        window = psum.tile([P, S], F32, name="window")
+        nc.tensor.matmul(window[:], identity[:], base_tile[:], start=True, stop=False)
+
+        for kb in range(KB):
+            nc.tensor.matmul(
+                window[:].indirect(offsets[:]),
+                w_tile[:, kb * M : (kb + 1) * M],
+                x_tile[:, kb * N : (kb + 1) * N],
+                start=False,
+                stop=(kb == KB - 1),
+            )
+
+        result = held.tile([P, S], F32, name="result")
+        nc.scalar.activation(result[:], window[:], TANH, bias=bias[:])
+        nc.sync.dma_start(out, result[:])

@@ -26,6 +26,10 @@ def tile_scatter_matmul_kernel(tc, base, x, w, b, offs, out):
         w_tile = held.tile([P, KB * M], BF16, name="w_tile")
         nc.scalar.dma_start(w_tile[:], w.rearrange("(p kb) m -> p (kb m)", kb=KB))
 
+        warm = held.tile([P, 1], F32, name="warm")
+        nc.vector.memset(warm[:], 0.0)
+        nc.scalar.activation(warm[:], warm[:], TANH)
+
         identity = held.tile([P, P], BF16, name="identity")
         make_identity(nc, identity[:])
 

@@ -13,18 +13,19 @@ TANH = mybir.ActivationFunctionType.Tanh
 def tile_scatter_matmul_kernel(tc, base, x, w, b, offs, out):
     nc = tc.nc
     with tc.tile_pool(name="held", bufs=1) as held, tc.psum_pool(name="psum", bufs=1) as psum:
-        offsets = held.tile([P, N // 16], U16, name="offsets")
-        nc.sync.dma_start(offsets[:], offs)
-
         base_tile = held.tile([P, S], BF16, name="base_tile")
         nc.scalar.dma_start(base_tile[:], base)
-        bias = held.tile([P, 1], F32, name="bias")
-        nc.scalar.dma_start(bias[:], b)
 
         x_tile = held.tile([P, KB * N], BF16, name="x_tile")
         nc.sync.dma_start(x_tile[:], x.rearrange("(p kb) n -> p (kb n)", kb=KB))
         w_tile = held.tile([P, KB * M], BF16, name="w_tile")
         nc.scalar.dma_start(w_tile[:], w.rearrange("(p kb) m -> p (kb m)", kb=KB))
+
+        offsets = held.tile([P, N // 16], U16, name="offsets")
+        nc.sync.dma_start(offsets[:], offs)
+
+        bias = held.tile([P, 1], F32, name="bias")
+        nc.sync.dma_start(bias[:], b)
 
         warm = held.tile([P, 1], F32, name="warm")
         nc.vector.memset(warm[:], 0.0)
@@ -46,5 +47,8 @@ def tile_scatter_matmul_kernel(tc, base, x, w, b, offs, out):
             )
 
         result = held.tile([P, S], F32, name="result")
-        nc.scalar.activation(result[:], window[:], TANH, bias=bias[:])
-        nc.sync.dma_start(out, result[:])
+        half = S // 2
+        for h, queue in enumerate((nc.sync, nc.scalar)):
+            columns = slice(h * half, (h + 1) * half)
+            nc.scalar.activation(result[:, columns], window[:, columns], TANH, bias=bias[:])
+            queue.dma_start(out[:, columns], result[:, columns])

@@ -5,6 +5,8 @@ P = 128
 S, K, M, N = 256, 512, 128, 128
 KB = K // P
 FLOPS = 2 * K * M * N
+BANK = 512
+WARM_MATMULS = 3
 
 BF16, F32, U16 = mybir.dt.bfloat16, mybir.dt.float32, mybir.dt.uint16
 TANH = mybir.ActivationFunctionType.Tanh
@@ -13,23 +15,28 @@ TANH = mybir.ActivationFunctionType.Tanh
 def tile_scatter_matmul_kernel(tc, base, x, w, b, offs, out):
     nc = tc.nc
     with tc.tile_pool(name="held", bufs=1) as held, tc.psum_pool(name="psum", bufs=1) as psum:
+        offsets = held.tile([P, N // 16], U16, name="offsets")
+        nc.sync.dma_start(offsets[:], offs)
+
         base_tile = held.tile([P, S], BF16, name="base_tile")
         nc.scalar.dma_start(base_tile[:], base)
+        bias = held.tile([P, 1], F32, name="bias")
+        nc.scalar.dma_start(bias[:], b)
 
         x_tile = held.tile([P, KB * N], BF16, name="x_tile")
         nc.sync.dma_start(x_tile[:], x.rearrange("(p kb) n -> p (kb n)", kb=KB))
         w_tile = held.tile([P, KB * M], BF16, name="w_tile")
         nc.scalar.dma_start(w_tile[:], w.rearrange("(p kb) m -> p (kb m)", kb=KB))
 
-        offsets = held.tile([P, N // 16], U16, name="offsets")
-        nc.sync.dma_start(offsets[:], offs)
+        zeros = held.tile([P, BANK], BF16, name="zeros")
+        nc.gpsimd.memset(zeros[:], 0.0)
 
-        bias = held.tile([P, 1], F32, name="bias")
-        nc.sync.dma_start(bias[:], b)
+        unread = psum.tile([P, BANK], F32, name="unread")
+        for i in range(WARM_MATMULS):
+            nc.tensor.matmul(unread[:], zeros[:, :P], zeros[:], start=True, stop=True)
 
-        warm = held.tile([P, 1], F32, name="warm")
-        nc.vector.memset(warm[:], 0.0)
-        nc.scalar.activation(warm[:], warm[:], TANH)
+        tanh_of_zero = held.tile([P, 1], F32, name="tanh_of_zero")
+        nc.scalar.activation(tanh_of_zero[:], zeros[:, 0:1], TANH)
 
         identity = held.tile([P, P], BF16, name="identity")
         make_identity(nc, identity[:])
@@ -47,8 +54,5 @@ def tile_scatter_matmul_kernel(tc, base, x, w, b, offs, out):
             )
 
         result = held.tile([P, S], F32, name="result")
-        half = S // 2
-        for h, queue in enumerate((nc.sync, nc.scalar)):
-            columns = slice(h * half, (h + 1) * half)
-            nc.scalar.activation(result[:, columns], window[:, columns], TANH, bias=bias[:])
-            queue.dma_start(out[:, columns], result[:, columns])
+        nc.scalar.activation(result[:], window[:], TANH, bias=bias[:])
+        nc.sync.dma_start(out, result[:])

@@ -4,6 +4,8 @@ from concourse.masks import make_identity
 P = 128
 S, K, M, N = 256, 512, 128, 128
 KB = K // P
+HALVES = 2
+BLOCKS_IN_HALF = KB // HALVES
 FLOPS = 2 * K * M * N
 BANK = 512
 WARM_MATMULS = 3
@@ -20,13 +22,19 @@ def tile_scatter_matmul_kernel(tc, base, x, w, b, offs, out):
 
         base_tile = held.tile([P, S], BF16, name="base_tile")
         nc.scalar.dma_start(base_tile[:], base)
-        bias = held.tile([P, 1], F32, name="bias")
-        nc.scalar.dma_start(bias[:], b)
 
-        x_tile = held.tile([P, KB * N], BF16, name="x_tile")
-        nc.sync.dma_start(x_tile[:], x.rearrange("(p kb) n -> p (kb n)", kb=KB))
-        w_tile = held.tile([P, KB * M], BF16, name="w_tile")
-        nc.scalar.dma_start(w_tile[:], w.rearrange("(p kb) m -> p (kb m)", kb=KB))
+        x_tiles, w_tiles = [], []
+        for h in range(HALVES):
+            rows = slice(h * K // HALVES, (h + 1) * K // HALVES)
+            x_tile = held.tile([P, BLOCKS_IN_HALF * N], BF16, name="x_tile%d" % h)
+            nc.sync.dma_start(x_tile[:], x[rows].rearrange("(p j) n -> p (j n)", j=BLOCKS_IN_HALF))
+            x_tiles.append(x_tile)
+            w_tile = held.tile([P, BLOCKS_IN_HALF * M], BF16, name="w_tile%d" % h)
+            nc.scalar.dma_start(w_tile[:], w[rows].rearrange("(p j) m -> p (j m)", j=BLOCKS_IN_HALF))
+            w_tiles.append(w_tile)
+
+        bias = held.tile([P, 1], F32, name="bias")
+        nc.sync.dma_start(bias[:], b)
 
         zeros = held.tile([P, BANK], BF16, name="zeros")
         nc.gpsimd.memset(zeros[:], 0.0)
@@ -45,10 +53,11 @@ def tile_scatter_matmul_kernel(tc, base, x, w, b, offs, out):
         nc.tensor.matmul(window[:], identity[:], base_tile[:], start=True, stop=False)
 
         for kb in range(KB):
+            h, j = divmod(kb, BLOCKS_IN_HALF)
             nc.tensor.matmul(
                 window[:].indirect(offsets[:]),
-                w_tile[:, kb * M : (kb + 1) * M],
-                x_tile[:, kb * N : (kb + 1) * N],
+                w_tiles[h][:, j * M : (j + 1) * M],
+                x_tiles[h][:, j * N : (j + 1) * N],
                 start=False,
                 stop=(kb == KB - 1),
             )

@@ -17,11 +17,12 @@ TANH = mybir.ActivationFunctionType.Tanh
 def tile_scatter_matmul_kernel(tc, base, x, w, b, offs, out):
     nc = tc.nc
     with tc.tile_pool(name="held", bufs=1) as held, tc.psum_pool(name="psum", bufs=1) as psum:
-        offsets = held.tile([P, N // 16], U16, name="offsets")
-        nc.sync.dma_start(offsets[:], offs)
 
         base_tile = held.tile([P, S], BF16, name="base_tile")
-        nc.scalar.dma_start(base_tile[:], base)
+        nc.sync.dma_start(base_tile[:], base)
+
+        offsets = held.tile([P, N // 16], U16, name="offsets")
+        nc.sync.dma_start(offsets[:], offs)
 
         x_tiles, w_tiles = [], []
         for h in range(HALVES):
@@ -30,7 +31,7 @@ def tile_scatter_matmul_kernel(tc, base, x, w, b, offs, out):
             nc.sync.dma_start(x_tile[:], x[rows].rearrange("(p j) n -> p (j n)", j=BLOCKS_IN_HALF))
             x_tiles.append(x_tile)
             w_tile = held.tile([P, BLOCKS_IN_HALF * M], BF16, name="w_tile%d" % h)
-            nc.scalar.dma_start(w_tile[:], w[rows].rearrange("(p j) m -> p (j m)", j=BLOCKS_IN_HALF))
+            nc.sync.dma_start(w_tile[:], w[rows].rearrange("(p j) m -> p (j m)", j=BLOCKS_IN_HALF))
             w_tiles.append(w_tile)
 
         bias = held.tile([P, 1], F32, name="bias")

@@ -37,12 +37,18 @@ def tile_scatter_matmul_kernel(tc, base, x, w, b, offs, out):
         bias = held.tile([P, 1], F32, name="bias")
         nc.sync.dma_start(bias[:], b)
 
-        zeros = held.tile([P, BANK], BF16, name="zeros")
-        nc.gpsimd.memset(zeros[:], 0.0)
+        zeros = held.tile([P, 2], BF16, name="zeros")
+        nc.vector.memset(zeros[:], 0.0)
 
         unread = psum.tile([P, BANK], F32, name="unread")
         for i in range(WARM_MATMULS):
-            nc.tensor.matmul(unread[:], zeros[:, :P], zeros[:], start=True, stop=True)
+            nc.tensor.matmul(
+                unread[:],
+                zeros[:, 0:1].to_broadcast([P, P]),
+                zeros[:, 0:1].to_broadcast([P, BANK]),
+                start=True,
+                stop=True,
+            )
 
         tanh_of_zero = held.tile([P, 1], F32, name="tanh_of_zero")
         nc.scalar.activation(tanh_of_zero[:], zeros[:, 0:1], TANH)

@@ -38,7 +38,7 @@ def tile_scatter_matmul_kernel(tc, base, x, w, b, offs, out):
         nc.sync.dma_start(bias[:], b)
 
         zeros = held.tile([P, 2], BF16, name="zeros")
-        nc.vector.memset(zeros[:], 0.0)
+        nc.gpsimd.memset(zeros[:], 0.0)
 
         unread = psum.tile([P, BANK], F32, name="unread")
         for i in range(WARM_MATMULS):

import concourse.mybir as mybir
from concourse.masks import make_identity

P = 128
S, K, M, N = 256, 512, 128, 128
KB = K // P
HALVES = 2
BLOCKS_IN_HALF = KB // HALVES
FLOPS = 2 * K * M * N
BANK = 512
WARM_MATMULS = 3

BF16, F32, U16 = mybir.dt.bfloat16, mybir.dt.float32, mybir.dt.uint16
TANH = mybir.ActivationFunctionType.Tanh


def tile_scatter_matmul_kernel(tc, base, x, w, b, offs, out):
    nc = tc.nc
    with tc.tile_pool(name="held", bufs=1) as held, tc.psum_pool(name="psum", bufs=1) as psum:

        base_tile = held.tile([P, S], BF16, name="base_tile")
        nc.sync.dma_start(base_tile[:], base)

        offsets = held.tile([P, N // 16], U16, name="offsets")
        nc.sync.dma_start(offsets[:], offs)

        x_tiles, w_tiles = [], []
        for h in range(HALVES):
            rows = slice(h * K // HALVES, (h + 1) * K // HALVES)
            x_tile = held.tile([P, BLOCKS_IN_HALF * N], BF16, name="x_tile%d" % h)
            nc.sync.dma_start(x_tile[:], x[rows].rearrange("(p j) n -> p (j n)", j=BLOCKS_IN_HALF))
            x_tiles.append(x_tile)
            w_tile = held.tile([P, BLOCKS_IN_HALF * M], BF16, name="w_tile%d" % h)
            nc.sync.dma_start(w_tile[:], w[rows].rearrange("(p j) m -> p (j m)", j=BLOCKS_IN_HALF))
            w_tiles.append(w_tile)

        bias = held.tile([P, 1], F32, name="bias")
        nc.sync.dma_start(bias[:], b)

        zeros = held.tile([P, 2], BF16, name="zeros")
        nc.gpsimd.memset(zeros[:], 0.0)

        unread = psum.tile([P, BANK], F32, name="unread")
        for i in range(WARM_MATMULS):
            nc.tensor.matmul(
                unread[:],
                zeros[:, 0:1].to_broadcast([P, P]),
                zeros[:, 0:1].to_broadcast([P, BANK]),
                start=True,
                stop=True,
            )

        tanh_of_zero = held.tile([P, 1], F32, name="tanh_of_zero")
        nc.scalar.activation(tanh_of_zero[:], zeros[:, 0:1], TANH)

        identity = held.tile([P, P], BF16, name="identity")
        make_identity(nc, identity[:])

        window = psum.tile([P, S], F32, name="window")
        nc.tensor.matmul(window[:], identity[:], base_tile[:], start=True, stop=False)

        for kb in range(KB):
            h, j = divmod(kb, BLOCKS_IN_HALF)
            nc.tensor.matmul(
                window[:].indirect(offsets[:]),
                w_tiles[h][:, j * M : (j + 1) * M],
                x_tiles[h][:, j * N : (j + 1) * N],
                start=False,
                stop=(kb == KB - 1),
            )

        result = held.tile([P, S], F32, name="result")
        nc.scalar.activation(result[:], window[:], TANH, bias=bias[:])
        nc.sync.dma_start(out, result[:])
